import numpy as np
import ml_dtypes


def mxq(x, axis, fmt="e4m3"):
    dtype, down = {"e4m3": (ml_dtypes.float8_e4m3fn, 7), "e5m2": (ml_dtypes.float8_e5m2, 14)}[fmt]
    v = np.moveaxis(np.asarray(x, np.float32).astype(ml_dtypes.bfloat16).astype(np.float64), axis, -1)
    blocks = v.reshape(v.shape[:-1] + (-1, 32))
    amax = np.abs(blocks).max(-1, keepdims=True)
    byte = np.maximum(np.where(amax > 0, np.frexp(amax)[1] - 1 + 127, 0) - down, 1)
    scale = np.exp2(byte - 127.0)
    codes = (blocks / scale).astype(np.float32).astype(dtype).astype(np.float64)
    return np.moveaxis((codes * scale).reshape(v.shape), -1, axis)


WIDE = False


def mx_kscale(k):
    if not WIDE:
        return np.ones(k)
    levels = np.array([10, -10, 5, -5, 0])
    if k % 512:
        return np.exp2(np.random.permutation(np.resize(levels, k // 32))).repeat(32)
    a = np.empty((k // 512, 16))
    for p in range(k // 512):
        a[p, :8] = np.random.permutation(np.resize(levels, 8))
        for g in range(8):
            far = levels[np.abs(levels - a[p, g]) >= 10]
            a[p, g + 8] = far[np.random.randint(len(far))]
    return np.exp2(a.ravel()).repeat(32)


def f64(x):
    return np.asarray(x).astype(np.float64)


def striped(idx):
    return np.tile(np.asarray(idx).reshape(-1, 16).T, (8, 1)).astype(np.uint16)


def unstriped(offs):
    return offs[:16].T.reshape(-1).astype(np.int64)


E2M1 = np.array([0.0, 0.5, 1.0, 1.5, 2.0, 3.0, 4.0, 6.0, -0.0, -0.5, -1.0, -1.5, -2.0, -3.0, -4.0, -6.0])


def pack_weight(w, fmt):
    k, n = w.shape
    w = f64(np.asarray(w, np.float32).astype(ml_dtypes.bfloat16)).reshape(k // 32, 32, n)
    amax = np.abs(w).max(1)
    if fmt == "e4m3":
        byte = np.frexp(amax)[1] - 1 + 127 - 7
    else:
        mant, ex = np.frexp(amax / 6.0)
        byte = np.where(mant > 0.5, ex, ex - 1) + 127
    byte = np.clip(np.where(amax > 0, byte, 1), 1, 254)
    scaled = (w * np.exp2(127.0 - byte)[:, None, :]).reshape(k, n).astype(np.float32)
    by_word = np.ascontiguousarray(scaled.reshape(k // 512, 128, 4, n).transpose(0, 1, 3, 2))
    if fmt == "e4m3":
        words = by_word.astype(ml_dtypes.float8_e4m3fn).view(np.uint8)
    else:
        c = by_word.astype(ml_dtypes.float4_e2m1fn).view(np.uint8) & 0xF
        words = (c[..., 0::2] | (c[..., 1::2] << 4)).reshape(k // 512, 128, 2 * n)
    return np.ascontiguousarray(words), np.ascontiguousarray(byte.astype(np.uint8).reshape(k // 512, 16, n))


def unpack_weight(words, scales, fmt):
    g, _, n = scales.shape
    words = np.ascontiguousarray(words).reshape(g, 128, n, -1)
    if fmt == "e4m3":
        vals = words.view(ml_dtypes.float8_e4m3fn).astype(np.float64)
    else:
        nib = np.empty((g, 128, n, 4), np.uint8)
        nib[..., 0::2] = words & 0xF
        nib[..., 1::2] = words >> 4
        vals = E2M1[nib]
    vals = vals * np.repeat(np.exp2(scales.astype(np.float64) - 127.0), 8, axis=1)[..., None]
    return vals.transpose(0, 1, 3, 2).reshape(g * 512, n)


def softplus(v):
    return np.log(1.0 + np.exp(v))


def sigmoid(v):
    return 1.0 / (1.0 + np.exp(-v))


D, E, T, I, Q, G = 512, 512, 2048, 512, 128, 64


def setup_inputs():
    n = np.random.standard_normal
    idx = np.random.permutation(T)[:I]
    fd = mx_kscale(D)
    fe = mx_kscale(E)
    keysp = pack_weight(n((D, T)) / fd[:, None], "e4m3")
    valsp = pack_weight(n((E, T)) / fe[:, None], "e4m3")
    return {
        "query": (n((D, Q)) * 0.8 / np.sqrt(D) * fd[:, None]).astype(np.float32),
        "query2": (n((D, Q)) * 1.0 / np.sqrt(D) * fd[:, None]).astype(np.float32),
        "keys_words": keysp[0],
        "keys_scales": keysp[1],
        "reserve": (np.random.uniform(2.0, 10.0, (Q, 1))).astype(np.float32),
        "gout": (n((E, Q)) * 1 / np.sqrt(E) * fe[:, None]).astype(np.float32),
        "vals_words": valsp[0],
        "vals_scales": valsp[1],
        "base": (0.5 * n((Q, I))).astype(np.float32),
        "offs": striped(idx),
    }


def reference(query, query2, keys_words, keys_scales, reserve, gout, vals_words, vals_scales, base, offs):
    idx = unstriped(offs)
    keysu = unpack_weight(keys_words, keys_scales, "e4m3")
    valsu = unpack_weight(vals_words, vals_scales, "e4m3")
    queryq = mxq(f64(query), 0, "e4m3")
    keysidxg = keysu[:, idx]
    a = queryq.T @ keysidxg
    query2q = mxq(f64(query2), 0, "e4m3")
    b = query2q.T @ keysidxg
    m1 = b.reshape(Q, G, I // G).mean(axis=2)
    q0 = softplus(m1 * 3.0)
    z = np.sum(q0, axis=1, keepdims=True) + f64(reserve)
    pa = np.exp(a)
    s = pa.reshape(Q, G, I // G).sum(axis=2)
    goutq = mxq(f64(gout), 0, "e4m3")
    valsidxg = valsu[:, idx]
    c0 = goutq.T @ valsidxg
    drr = c0 * pa
    dr = drr.reshape(Q, G, I // G).sum(axis=2)
    dz = np.sum(dr * q0 / s / np.square(z) * (-1.0), axis=1, keepdims=True)
    dq0 = dr / z / s + dz
    dm1 = dq0 * sigmoid(m1 * 3.0) * 3.0
    e1 = dm1 / 8.0
    r1 = np.repeat(e1, I // G, axis=1)
    hr1 = r1 * 1024.0 * 2.0 * 1024.0
    he1 = hr1.reshape(Q, G, I // G).sum(axis=2)
    hdm1 = he1 / 8.0
    hdq0 = hdm1 * 3.0 * sigmoid(m1 * 3.0)
    hdz = np.sum(hdq0, axis=1, keepdims=True)
    hz = np.sum(hdq0 / s * dr / np.square(z) * (-1.0), axis=1, keepdims=True) + np.sum(hdz * (-1.0) * dr * q0 / s / np.square(np.square(z)) * (-1.0), axis=1, keepdims=True) * z * 2.0
    hq0 = hdz * (-1.0) / np.square(z) * dr / s + hz
    hm1 = hdm1 * 3.0 * dq0 * sigmoid(m1 * 3.0) * (1.0 - sigmoid(m1 * 3.0)) * 3.0 + hq0 * sigmoid(m1 * 3.0) * 3.0
    e51 = hm1 / 8.0
    r51 = np.repeat(e51, I // G, axis=1)
    y = r51 + f64(base)
    return y

@@ -1,0 +1,214 @@
+import math
+from contextlib import ExitStack
+
+import concourse.mybir as mybir
+
+D, E, T, I, Q, G = 512, 512, 2048, 512, 128, 64
+PAGE = I // G
+FLOPS = 3 * 2 * D * Q * I
+
+F32 = mybir.dt.float32
+BF16 = mybir.dt.bfloat16
+I32 = mybir.dt.int32
+U32 = mybir.dt.uint32
+U16 = mybir.dt.uint16
+U8 = mybir.dt.uint8
+FP8X4 = mybir.dt.float8_e4m3fn_x4
+ALU = mybir.AluOpType
+ACT = mybir.ActivationFunctionType
+AXIS_X = mybir.AxisListType.X
+
+P = 128
+PACK = 4
+KIB = 1024
+GAIN = 9.0 * (1024.0 * 2.0 * 1024.0 * 3.0 / 8.0) / 8.0
+SLOT_HALVES = (slice(0, I // 2), slice(I // 2, I))
+PAGE_HALVES = (slice(0, G // 2), slice(G // 2, G))
+LIST_HALVES = (slice(0, I // 32), slice(I // 32, I // 16))
+
+
+def tile_attend_gppagequotas_kernel(
+    tc, query, query2, keys_words, keys_scales, reserve, gout, vals_words, vals_scales, base, offs, out
+):
+    nc = tc.nc
+    with ExitStack() as ctx:
+        sb = ctx.enter_context(tc.tile_pool(name="sb", bufs=1))
+        shared = ctx.enter_context(tc.tile_pool(name="shared", bufs=1))
+        ps = ctx.enter_context(tc.psum_pool(name="ps", bufs=1))
+
+        def pages(ap):
+            return ap.rearrange("p (g j) -> p g j", j=PAGE)
+
+        def spread(ap):
+            return ap.rearrange("p (g o) -> p g o", o=1).to_broadcast([P, ap.shape[1], PAGE])
+
+        def placed(shape, dtype, name, kib):
+            return shared.tile(shape, dtype, name=name, offset=int(kib * KIB), align_bytes=64)
+
+        def small(name, width=G):
+            return sb.tile([P, width], F32, name=name)
+
+        def load_words(words, pool_words):
+            nc.sync.dma_start(words[:], pool_words[0].rearrange("p n t -> p (n t)").bitcast(I32))
+
+        def load_scales(plane, pool_scales, zeroer, queues):
+            zeroer.memset(plane[:].bitcast(I32), 0)
+            for r, queue in enumerate(queues):
+                queue.dma_start(plane[r:P:32, :].bitcast(I32), pool_scales[0][r:16:4, :].bitcast(I32))
+
+        def load_rows(raw, rows):
+            nc.sync.dma_start(raw[:], rows.rearrange("(p j) q -> p j q", j=PACK))
+
+        def round_on_scalar(grouped, raw):
+            nc.scalar.copy(grouped, raw)
+
+        def round_on_gpsimd(grouped, raw):
+            nc.gpsimd.tensor_scalar(grouped, raw, 1.0, 0.0, ALU.mult, ALU.add)
+
+        def quantise(raw, grouped, name, rounder):
+            rounder(grouped[:], raw[:].rearrange("p j q -> p q j"))
+            codes = sb.tile([P, Q], U32, name=name + "_codes", align_bytes=64)
+            scales = sb.tile([P, Q], U8, name=name + "_scales", align_bytes=64)
+            nc.vector.quantize_mx(codes[:].bitcast(FP8X4), scales[:], grouped[:].rearrange("p q j -> p (q j)"))
+            return codes, scales
+
+        def gather(picked, window, dtype, entries):
+            nc.vector.tensor_copy(picked, window[:].bitcast(dtype).indirect(entries))
+
+        def product(acc, rows, words, scales):
+            nc.tensor.matmul_mx(
+                acc, lhsT=rows[0][:].bitcast(FP8X4), lhsT_scale=rows[1][:],
+                rhs=words.bitcast(FP8X4), rhs_scale=scales, start=True, stop=True,
+            )
+
+        offsets = sb.tile([P, I // 16], U16, name="offsets")
+        nc.sync.dma_start(offsets[:], offs)
+        key_plane = placed([P, T], U8, "key_plane", 7)
+        load_scales(key_plane, keys_scales, nc.vector, [nc.scalar] * 4)
+        q_raw = sb.tile([P, PACK, Q], F32, name="q_raw")
+        load_rows(q_raw, query)
+        key_pool = placed([P, T], I32, "key_pool", 10)
+        load_words(key_pool, keys_words)
+        q2_raw = sb.tile([P, PACK, Q], F32, name="q2_raw")
+        load_rows(q2_raw, query2)
+        val_plane = sb.tile([P, T], U8, name="val_plane", align_bytes=64)
+        load_scales(val_plane, vals_scales, nc.gpsimd, [nc.gpsimd, nc.gpsimd, nc.scalar, nc.scalar])
+        half = small("half", 1)
+        nc.gpsimd.memset(half[:], 0.5)
+        quarter = small("quarter", 1)
+        nc.gpsimd.memset(quarter[:], 0.25)
+
+        key_scales = sb.tile([P, I], U8, name="key_scales", align_bytes=64)
+        gather(key_scales[:], key_plane, U8, offsets[:])
+        val_pool = placed([P, T], I32, "val_pool", 0)
+        load_words(val_pool, vals_words)
+        q_mx = quantise(q_raw, placed([P, Q, PACK], BF16, "q_bf", 18), "q", round_on_scalar)
+        key_words = [placed([P, I // 2], U32, "key_words%d" % h, 8 + h) for h in range(2)]
+        a_ps = [ps.tile([Q, I // 2], F32, name="a_ps%d" % h) for h in range(2)]
+        for h in range(2):
+            gather(key_words[h][:], key_pool, U32, offsets[:, LIST_HALVES[h]])
+            product(a_ps[h][:], q_mx, key_words[h][:], key_scales[:, SLOT_HALVES[h]])
+        g_raw = placed([P, PACK, Q], F32, "g_raw", 10)
+        load_rows(g_raw, gout)
+        base_sb = placed([P, I], F32, "base_sb", 12)
+        nc.sync.dma_start(base_sb[:], base)
+        reserve_sb = placed([P, 1], F32, "reserve_sb", 14)
+        nc.sync.dma_start(reserve_sb[:], reserve)
+        q2_mx = quantise(q2_raw, placed([P, Q, PACK], BF16, "q2_bf", 19), "q2", round_on_scalar)
+        b_ps = ps.tile([Q, I], F32, name="b_ps")
+        for h in range(2):
+            product(b_ps[:, SLOT_HALVES[h]], q2_mx, key_words[h][:], key_scales[:, SLOT_HALVES[h]])
+
+        page_max = sb.tile([P, G], F32, name="page_max", tag="max_then_scales", align_bytes=64)
+        shifted = sb.tile([P, I], F32, name="shifted", tag="shifted_then_words", align_bytes=64)
+        pa = sb.tile([P, I], F32, name="pa")
+        for h in range(2):
+            nc.vector.tensor_reduce(page_max[:, PAGE_HALVES[h]], pages(a_ps[h][:]), AXIS_X, ALU.max)
+        for h in range(2):
+            nc.vector.tensor_tensor(
+                pages(shifted[:, SLOT_HALVES[h]]), pages(a_ps[h][:]), spread(page_max[:, PAGE_HALVES[h]]), ALU.subtract
+            )
+            nc.scalar.activation(pa[:, SLOT_HALVES[h]], shifted[:, SLOT_HALVES[h]], ACT.Exp)
+
+        b_sum = small("b_sum")
+        nc.vector.tensor_reduce(b_sum[:], pages(b_ps[:]), AXIS_X, ALU.add)
+        th = small("th")
+        nc.scalar.activation(th[:], b_sum[:], ACT.Tanh, scale=3.0 / 16.0)
+        pos = small("pos")
+        pos_sum = small("pos_sum", 1)
+        nc.scalar.activation(pos[:], b_sum[:], ACT.Relu, scale=3.0 / 8.0, accum_out=pos_sum[:])
+        th_abs = small("th_abs")
+        nc.scalar.activation(th_abs[:], th[:], ACT.Abs)
+        log_sig = small("log_sig")
+        log_sum = small("log_sum", 1)
+        nc.scalar.activation(log_sig[:], th_abs[:], ACT.Ln, bias=half[:], scale=0.5, accum_out=log_sum[:])
+        sig_sq = small("sig_sq")
+        sig_sq_sum = small("sig_sq_sum", 1)
+        nc.scalar.activation(sig_sq[:], th[:], ACT.Square, bias=half[:], scale=0.5, accum_out=sig_sq_sum[:])
+        sig = small("sig")
+        nc.scalar.activation(sig[:], th[:], ACT.Identity, bias=half[:], scale=0.5)
+        th_sq = small("th_sq")
+        nc.scalar.activation(th_sq[:], th[:], ACT.Square, scale=0.5)
+        slope = small("slope")
+        nc.scalar.activation(slope[:], th_sq[:], ACT.Identity, bias=quarter[:], scale=-1.0)
+
+        val_scales = sb.tile([P, I], U8, name="val_scales", tag="max_then_scales", align_bytes=64)
+        gather(val_scales[:], val_plane, U8, offsets[:])
+        val_words = sb.tile([P, I], U32, name="val_words", tag="shifted_then_words", align_bytes=64)
+        gather(val_words[:], val_pool, U32, offsets[:])
+        g_mx = quantise(g_raw, placed([P, Q, PACK], BF16, "g_bf", 20), "g", round_on_gpsimd)
+        c_ps = ps.tile([Q, I], F32, name="c_ps")
+        product(c_ps[:], g_mx, val_words[:], val_scales[:])
+
+        s = placed([P, G], F32, "s", 20)
+        nc.vector.tensor_reduce(s[:], pages(pa[:]), AXIS_X, ALU.add)
+        neg_z = placed([P, 1], F32, "neg_z", 20.25)
+        nc.vector.tensor_scalar(neg_z[:], log_sum[:], pos_sum[:], reserve_sb[:], ALU.subtract, ALU.subtract)
+        inv_s = small("inv_s")
+        nc.vector.reciprocal(inv_s[:], s[:])
+        drr = sb.tile([P, I], F32, name="drr")
+        nc.vector.tensor_tensor(drr[:], c_ps[:], pa[:], ALU.mult)
+        q0 = placed([P, G], F32, "q0", 20.5)
+        nc.vector.tensor_tensor(q0[:], pos[:], log_sig[:], ALU.subtract)
+        neg_inv_z = small("neg_inv_z", 1)
+        nc.vector.reciprocal(neg_inv_z[:], neg_z[:])
+        dr = small("dr")
+        nc.vector.tensor_reduce(dr[:], pages(drr[:]), AXIS_X, ALU.add)
+        q0_s = small("q0_s")
+        nc.vector.tensor_tensor(q0_s[:], q0[:], inv_s[:], ALU.mult)
+        sig_sq_s = small("sig_sq_s")
+        nc.vector.tensor_tensor(sig_sq_s[:], sig_sq[:], inv_s[:], ALU.mult)
+        neg_p = small("neg_p", 1)
+        nc.scalar.activation(neg_p[:], sig_sq_sum[:], ACT.Copy, scale=neg_inv_z[:])
+        gain = small("gain", 1)
+        nc.scalar.activation(gain[:], neg_inv_z[:], ACT.Square, scale=math.sqrt(GAIN))
+
+        terms = small("terms")
+        neg_mu = small("neg_mu", 1)
+        nc.vector.scalar_tensor_tensor(terms[:], dr[:], neg_inv_z[:], q0_s[:], ALU.mult, ALU.mult, accum_out=neg_mu[:])
+        u = small("u")
+        nc.vector.tensor_tensor(u[:], dr[:], inv_s[:], ALU.mult)
+        terms2 = small("terms2")
+        neg_b = small("neg_b", 1)
+        nc.vector.scalar_tensor_tensor(terms2[:], dr[:], neg_inv_z[:], sig_sq_s[:], ALU.mult, ALU.mult, accum_out=neg_b[:])
+        v = small("v")
+        nc.vector.scalar_tensor_tensor(v[:], u[:], neg_mu[:], sig[:], ALU.add, ALU.mult)
+        vo = small("vo")
+        nc.vector.scalar_tensor_tensor(vo[:], u[:], neg_mu[:], slope[:], ALU.add, ALU.mult)
+        neg_s1 = small("neg_s1", 1)
+        nc.vector.tensor_scalar(neg_s1[:], neg_p[:], neg_mu[:], neg_b[:], ALU.mult, ALU.add)
+        terms3 = small("terms3")
+        neg_s2 = small("neg_s2", 1)
+        nc.vector.scalar_tensor_tensor(terms3[:], v[:], neg_inv_z[:], v[:], ALU.mult, ALU.mult, accum_out=neg_s2[:])
+        own = small("own")
+        nc.vector.scalar_tensor_tensor(own[:], vo[:], neg_s1[:], v[:], ALU.add, ALU.mult)
+        e = small("e")
+        nc.vector.scalar_tensor_tensor(e[:], sig[:], neg_s2[:], own[:], ALU.mult, ALU.add)
+
+        for h, queue in enumerate((nc.sync, nc.scalar)):
+            result = sb.tile([P, I // 2], F32, name="result%d" % h)
+            nc.vector.scalar_tensor_tensor(
+                pages(result[:]), spread(e[:, PAGE_HALVES[h]]), gain[:],
+                pages(base_sb[:, SLOT_HALVES[h]]), ALU.mult, ALU.add,
+            )
+            queue.dma_start(out[:, SLOT_HALVES[h]], result[:])

@@ -51,22 +51,18 @@ def tile_attend_gppagequotas_kernel(
         def load_words(words, pool_words):
             nc.sync.dma_start(words[:], pool_words[0].rearrange("p n t -> p (n t)").bitcast(I32))
 
-        def load_scales(plane, pool_scales, zeroer, queues):
-            zeroer.memset(plane[:].bitcast(I32), 0)
-            for r, queue in enumerate(queues):
-                queue.dma_start(plane[r:P:32, :].bitcast(I32), pool_scales[0][r:16:4, :].bitcast(I32))
+        def load_scales(plane, pool_scales):
+            nc.vector.memset(plane[:, : T // 2].bitcast(I32), 0)
+            nc.gpsimd.memset(plane[:, T // 2 :].bitcast(I32), 0)
+            for r in range(4):
+                nc.sync.dma_start(plane[r:P:32, :].bitcast(I32), pool_scales[0][r:16:4, :].bitcast(I32))
 
         def load_rows(raw, rows):
             nc.sync.dma_start(raw[:], rows.rearrange("(p j) q -> p j q", j=PACK))
 
-        def round_on_scalar(grouped, raw):
-            nc.scalar.copy(grouped, raw)
-
-        def round_on_gpsimd(grouped, raw):
-            nc.gpsimd.tensor_scalar(grouped, raw, 1.0, 0.0, ALU.mult, ALU.add)
-
-        def quantise(raw, grouped, name, rounder):
-            rounder(grouped[:], raw[:].rearrange("p j q -> p q j"))
+        def quantise(raw, name, tag):
+            grouped = sb.tile([P, Q, PACK], BF16, name=name + "_bf", tag=tag, align_bytes=64)
+            nc.scalar.copy(grouped[:], raw[:].rearrange("p j q -> p q j"))
             codes = sb.tile([P, Q], U32, name=name + "_codes", align_bytes=64)
             scales = sb.tile([P, Q], U8, name=name + "_scales", align_bytes=64)
             nc.vector.quantize_mx(codes[:].bitcast(FP8X4), scales[:], grouped[:].rearrange("p q j -> p (q j)"))
@@ -83,45 +79,46 @@ def tile_attend_gppagequotas_kernel(
 
         offsets = sb.tile([P, I // 16], U16, name="offsets")
         nc.sync.dma_start(offsets[:], offs)
-        key_plane = placed([P, T], U8, "key_plane", 7)
-        load_scales(key_plane, keys_scales, nc.vector, [nc.scalar] * 4)
+        key_plane = sb.tile([P, T], U8, name="key_plane", align_bytes=64)
+        load_scales(key_plane, keys_scales)
+        reserve_sb = small("reserve_sb", 1)
+        nc.sync.dma_start(reserve_sb[:], reserve)
         q_raw = sb.tile([P, PACK, Q], F32, name="q_raw")
         load_rows(q_raw, query)
-        key_pool = placed([P, T], I32, "key_pool", 10)
-        load_words(key_pool, keys_words)
         q2_raw = sb.tile([P, PACK, Q], F32, name="q2_raw")
         load_rows(q2_raw, query2)
-        val_plane = sb.tile([P, T], U8, name="val_plane", align_bytes=64)
-        load_scales(val_plane, vals_scales, nc.gpsimd, [nc.gpsimd, nc.gpsimd, nc.scalar, nc.scalar])
+        key_pool = sb.tile([P, T], I32, name="key_pool", align_bytes=64)
+        load_words(key_pool, keys_words)
+        g_raw = placed([P, PACK, Q], F32, "g_raw", 0)
+        load_rows(g_raw, gout)
+        val_pool = placed([P, T], I32, "val_pool", 3)
+        load_words(val_pool, vals_words)
+        val_plane = placed([P, T], U8, "val_plane", 15)
+        load_scales(val_plane, vals_scales)
+        base_sb = sb.tile([P, I], F32, name="base_sb")
+        nc.sync.dma_start(base_sb[:], base)
         half = small("half", 1)
-        nc.gpsimd.memset(half[:], 0.5)
+        nc.vector.memset(half[:], 0.5)
         quarter = small("quarter", 1)
-        nc.gpsimd.memset(quarter[:], 0.25)
+        nc.vector.memset(quarter[:], 0.25)
 
+        q_mx = quantise(q_raw, "q", "q_bf")
         key_scales = sb.tile([P, I], U8, name="key_scales", align_bytes=64)
         gather(key_scales[:], key_plane, U8, offsets[:])
-        val_pool = placed([P, T], I32, "val_pool", 0)
-        load_words(val_pool, vals_words)
-        q_mx = quantise(q_raw, placed([P, Q, PACK], BF16, "q_bf", 18), "q", round_on_scalar)
-        key_words = [placed([P, I // 2], U32, "key_words%d" % h, 8 + h) for h in range(2)]
+        q2_mx = quantise(q2_raw, "q2", "max_then_scales")
+        key_words = [sb.tile([P, I // 2], U32, name="key_words%d" % h, align_bytes=64) for h in range(2)]
         a_ps = [ps.tile([Q, I // 2], F32, name="a_ps%d" % h) for h in range(2)]
         for h in range(2):
             gather(key_words[h][:], key_pool, U32, offsets[:, LIST_HALVES[h]])
             product(a_ps[h][:], q_mx, key_words[h][:], key_scales[:, SLOT_HALVES[h]])
-        g_raw = placed([P, PACK, Q], F32, "g_raw", 10)
-        load_rows(g_raw, gout)
-        base_sb = placed([P, I], F32, "base_sb", 12)
-        nc.sync.dma_start(base_sb[:], base)
-        reserve_sb = placed([P, 1], F32, "reserve_sb", 14)
-        nc.sync.dma_start(reserve_sb[:], reserve)
-        q2_mx = quantise(q2_raw, placed([P, Q, PACK], BF16, "q2_bf", 19), "q2", round_on_scalar)
+        g_mx = quantise(g_raw, "g", "g_bf")
         b_ps = ps.tile([Q, I], F32, name="b_ps")
         for h in range(2):
             product(b_ps[:, SLOT_HALVES[h]], q2_mx, key_words[h][:], key_scales[:, SLOT_HALVES[h]])
 
         page_max = sb.tile([P, G], F32, name="page_max", tag="max_then_scales", align_bytes=64)
-        shifted = sb.tile([P, I], F32, name="shifted", tag="shifted_then_words", align_bytes=64)
-        pa = sb.tile([P, I], F32, name="pa")
+        shifted = placed([P, I], F32, "shifted", 12.25)
+        pa = placed([P, I], F32, "pa", 0.25)
         for h in range(2):
             nc.vector.tensor_reduce(page_max[:, PAGE_HALVES[h]], pages(a_ps[h][:]), AXIS_X, ALU.max)
         for h in range(2):
@@ -132,14 +129,14 @@ def tile_attend_gppagequotas_kernel(
 
         b_sum = small("b_sum")
         nc.vector.tensor_reduce(b_sum[:], pages(b_ps[:]), AXIS_X, ALU.add)
-        th = small("th")
+        th = placed([P, G], F32, "th", 0)
         nc.scalar.activation(th[:], b_sum[:], ACT.Tanh, scale=3.0 / 16.0)
         pos = small("pos")
         pos_sum = small("pos_sum", 1)
         nc.scalar.activation(pos[:], b_sum[:], ACT.Relu, scale=3.0 / 8.0, accum_out=pos_sum[:])
         th_abs = small("th_abs")
         nc.scalar.activation(th_abs[:], th[:], ACT.Abs)
-        log_sig = small("log_sig")
+        log_sig = placed([P, G], F32, "log_sig", 14)
         log_sum = small("log_sum", 1)
         nc.scalar.activation(log_sig[:], th_abs[:], ACT.Ln, bias=half[:], scale=0.5, accum_out=log_sum[:])
         sig_sq = small("sig_sq")
@@ -152,23 +149,22 @@ def tile_attend_gppagequotas_kernel(
         slope = small("slope")
         nc.scalar.activation(slope[:], th_sq[:], ACT.Identity, bias=quarter[:], scale=-1.0)
 
+        val_words = placed([P, I], U32, "val_words", 12)
+        gather(val_words[:], val_pool, U32, offsets[:])
         val_scales = sb.tile([P, I], U8, name="val_scales", tag="max_then_scales", align_bytes=64)
         gather(val_scales[:], val_plane, U8, offsets[:])
-        val_words = sb.tile([P, I], U32, name="val_words", tag="shifted_then_words", align_bytes=64)
-        gather(val_words[:], val_pool, U32, offsets[:])
-        g_mx = quantise(g_raw, placed([P, Q, PACK], BF16, "g_bf", 20), "g", round_on_gpsimd)
         c_ps = ps.tile([Q, I], F32, name="c_ps")
         product(c_ps[:], g_mx, val_words[:], val_scales[:])
 
-        s = placed([P, G], F32, "s", 20)
+        s = placed([P, G], F32, "s", 15)
         nc.vector.tensor_reduce(s[:], pages(pa[:]), AXIS_X, ALU.add)
-        neg_z = placed([P, 1], F32, "neg_z", 20.25)
+        neg_z = placed([P, 1], F32, "neg_z", 15.25)
         nc.vector.tensor_scalar(neg_z[:], log_sum[:], pos_sum[:], reserve_sb[:], ALU.subtract, ALU.subtract)
         inv_s = small("inv_s")
         nc.vector.reciprocal(inv_s[:], s[:])
         drr = sb.tile([P, I], F32, name="drr")
         nc.vector.tensor_tensor(drr[:], c_ps[:], pa[:], ALU.mult)
-        q0 = placed([P, G], F32, "q0", 20.5)
+        q0 = placed([P, G], F32, "q0", 15.5)
         nc.vector.tensor_tensor(q0[:], pos[:], log_sig[:], ALU.subtract)
         neg_inv_z = small("neg_inv_z", 1)
         nc.vector.reciprocal(neg_inv_z[:], neg_z[:])

import math
from contextlib import ExitStack

import concourse.mybir as mybir

D, E, T, I, Q, G = 512, 512, 2048, 512, 128, 64
PAGE = I // G
FLOPS = 3 * 2 * D * Q * I

F32 = mybir.dt.float32
BF16 = mybir.dt.bfloat16
I32 = mybir.dt.int32
U32 = mybir.dt.uint32
U16 = mybir.dt.uint16
U8 = mybir.dt.uint8
FP8X4 = mybir.dt.float8_e4m3fn_x4
ALU = mybir.AluOpType
ACT = mybir.ActivationFunctionType
AXIS_X = mybir.AxisListType.X

P = 128
PACK = 4
KIB = 1024
GAIN = 9.0 * (1024.0 * 2.0 * 1024.0 * 3.0 / 8.0) / 8.0
SLOT_HALVES = (slice(0, I // 2), slice(I // 2, I))
PAGE_HALVES = (slice(0, G // 2), slice(G // 2, G))
LIST_HALVES = (slice(0, I // 32), slice(I // 32, I // 16))


def tile_attend_gppagequotas_kernel(
    tc, query, query2, keys_words, keys_scales, reserve, gout, vals_words, vals_scales, base, offs, out
):
    nc = tc.nc
    with ExitStack() as ctx:
        sb = ctx.enter_context(tc.tile_pool(name="sb", bufs=1))
        shared = ctx.enter_context(tc.tile_pool(name="shared", bufs=1))
        ps = ctx.enter_context(tc.psum_pool(name="ps", bufs=1))

        def pages(ap):
            return ap.rearrange("p (g j) -> p g j", j=PAGE)

        def spread(ap):
            return ap.rearrange("p (g o) -> p g o", o=1).to_broadcast([P, ap.shape[1], PAGE])

        def placed(shape, dtype, name, kib):
            return shared.tile(shape, dtype, name=name, offset=int(kib * KIB), align_bytes=64)

        def small(name, width=G):
            return sb.tile([P, width], F32, name=name)

        def load_words(words, pool_words):
            nc.sync.dma_start(words[:], pool_words[0].rearrange("p n t -> p (n t)").bitcast(I32))

        def load_scales(plane, pool_scales):
            nc.vector.memset(plane[:, : T // 2].bitcast(I32), 0)
            nc.gpsimd.memset(plane[:, T // 2 :].bitcast(I32), 0)
            for r in range(4):
                nc.sync.dma_start(plane[r:P:32, :].bitcast(I32), pool_scales[0][r:16:4, :].bitcast(I32))

        def load_rows(raw, rows):
            nc.sync.dma_start(raw[:], rows.rearrange("(p j) q -> p j q", j=PACK))

        def quantise(raw, name, tag):
            grouped = sb.tile([P, Q, PACK], BF16, name=name + "_bf", tag=tag, align_bytes=64)
            nc.scalar.copy(grouped[:], raw[:].rearrange("p j q -> p q j"))
            codes = sb.tile([P, Q], U32, name=name + "_codes", align_bytes=64)
            scales = sb.tile([P, Q], U8, name=name + "_scales", align_bytes=64)
            nc.vector.quantize_mx(codes[:].bitcast(FP8X4), scales[:], grouped[:].rearrange("p q j -> p (q j)"))
            return codes, scales

        def gather(picked, window, dtype, entries):
            nc.vector.tensor_copy(picked, window[:].bitcast(dtype).indirect(entries))

        def product(acc, rows, words, scales):
            nc.tensor.matmul_mx(
                acc, lhsT=rows[0][:].bitcast(FP8X4), lhsT_scale=rows[1][:],
                rhs=words.bitcast(FP8X4), rhs_scale=scales, start=True, stop=True,
            )

        offsets = sb.tile([P, I // 16], U16, name="offsets")
        nc.sync.dma_start(offsets[:], offs)
        key_plane = sb.tile([P, T], U8, name="key_plane", align_bytes=64)
        load_scales(key_plane, keys_scales)
        reserve_sb = small("reserve_sb", 1)
        nc.sync.dma_start(reserve_sb[:], reserve)
        q_raw = sb.tile([P, PACK, Q], F32, name="q_raw")
        load_rows(q_raw, query)
        q2_raw = sb.tile([P, PACK, Q], F32, name="q2_raw")
        load_rows(q2_raw, query2)
        key_pool = sb.tile([P, T], I32, name="key_pool", align_bytes=64)
        load_words(key_pool, keys_words)
        g_raw = placed([P, PACK, Q], F32, "g_raw", 0)
        load_rows(g_raw, gout)
        val_pool = placed([P, T], I32, "val_pool", 3)
        load_words(val_pool, vals_words)
        val_plane = placed([P, T], U8, "val_plane", 15)
        load_scales(val_plane, vals_scales)
        base_sb = sb.tile([P, I], F32, name="base_sb")
        nc.sync.dma_start(base_sb[:], base)
        half = small("half", 1)
        nc.vector.memset(half[:], 0.5)
        quarter = small("quarter", 1)
        nc.vector.memset(quarter[:], 0.25)

        q_mx = quantise(q_raw, "q", "q_bf")
        key_scales = sb.tile([P, I], U8, name="key_scales", align_bytes=64)
        gather(key_scales[:], key_plane, U8, offsets[:])
        q2_mx = quantise(q2_raw, "q2", "max_then_scales")
        key_words = [sb.tile([P, I // 2], U32, name="key_words%d" % h, align_bytes=64) for h in range(2)]
        a_ps = [ps.tile([Q, I // 2], F32, name="a_ps%d" % h) for h in range(2)]
        for h in range(2):
            gather(key_words[h][:], key_pool, U32, offsets[:, LIST_HALVES[h]])
            product(a_ps[h][:], q_mx, key_words[h][:], key_scales[:, SLOT_HALVES[h]])
        g_mx = quantise(g_raw, "g", "g_bf")
        b_ps = ps.tile([Q, I], F32, name="b_ps")
        for h in range(2):
            product(b_ps[:, SLOT_HALVES[h]], q2_mx, key_words[h][:], key_scales[:, SLOT_HALVES[h]])

        page_max = sb.tile([P, G], F32, name="page_max", tag="max_then_scales", align_bytes=64)
        shifted = placed([P, I], F32, "shifted", 12.25)
        pa = placed([P, I], F32, "pa", 0.25)
        for h in range(2):
            nc.vector.tensor_reduce(page_max[:, PAGE_HALVES[h]], pages(a_ps[h][:]), AXIS_X, ALU.max)
        for h in range(2):
            nc.vector.tensor_tensor(
                pages(shifted[:, SLOT_HALVES[h]]), pages(a_ps[h][:]), spread(page_max[:, PAGE_HALVES[h]]), ALU.subtract
            )
            nc.scalar.activation(pa[:, SLOT_HALVES[h]], shifted[:, SLOT_HALVES[h]], ACT.Exp)

        b_sum = small("b_sum")
        nc.vector.tensor_reduce(b_sum[:], pages(b_ps[:]), AXIS_X, ALU.add)
        th = placed([P, G], F32, "th", 0)
        nc.scalar.activation(th[:], b_sum[:], ACT.Tanh, scale=3.0 / 16.0)
        pos = small("pos")
        pos_sum = small("pos_sum", 1)
        nc.scalar.activation(pos[:], b_sum[:], ACT.Relu, scale=3.0 / 8.0, accum_out=pos_sum[:])
        th_abs = small("th_abs")
        nc.scalar.activation(th_abs[:], th[:], ACT.Abs)
        log_sig = placed([P, G], F32, "log_sig", 14)
        log_sum = small("log_sum", 1)
        nc.scalar.activation(log_sig[:], th_abs[:], ACT.Ln, bias=half[:], scale=0.5, accum_out=log_sum[:])
        sig_sq = small("sig_sq")
        sig_sq_sum = small("sig_sq_sum", 1)
        nc.scalar.activation(sig_sq[:], th[:], ACT.Square, bias=half[:], scale=0.5, accum_out=sig_sq_sum[:])
        sig = small("sig")
        nc.scalar.activation(sig[:], th[:], ACT.Identity, bias=half[:], scale=0.5)
        th_sq = small("th_sq")
        nc.scalar.activation(th_sq[:], th[:], ACT.Square, scale=0.5)
        slope = small("slope")
        nc.scalar.activation(slope[:], th_sq[:], ACT.Identity, bias=quarter[:], scale=-1.0)

        val_words = placed([P, I], U32, "val_words", 12)
        gather(val_words[:], val_pool, U32, offsets[:])
        val_scales = sb.tile([P, I], U8, name="val_scales", tag="max_then_scales", align_bytes=64)
        gather(val_scales[:], val_plane, U8, offsets[:])
        c_ps = ps.tile([Q, I], F32, name="c_ps")
        product(c_ps[:], g_mx, val_words[:], val_scales[:])

        s = placed([P, G], F32, "s", 15)
        nc.vector.tensor_reduce(s[:], pages(pa[:]), AXIS_X, ALU.add)
        neg_z = placed([P, 1], F32, "neg_z", 15.25)
        nc.vector.tensor_scalar(neg_z[:], log_sum[:], pos_sum[:], reserve_sb[:], ALU.subtract, ALU.subtract)
        inv_s = small("inv_s")
        nc.vector.reciprocal(inv_s[:], s[:])
        drr = sb.tile([P, I], F32, name="drr")
        nc.vector.tensor_tensor(drr[:], c_ps[:], pa[:], ALU.mult)
        q0 = placed([P, G], F32, "q0", 15.5)
        nc.vector.tensor_tensor(q0[:], pos[:], log_sig[:], ALU.subtract)
        neg_inv_z = small("neg_inv_z", 1)
        nc.vector.reciprocal(neg_inv_z[:], neg_z[:])
        dr = small("dr")
        nc.vector.tensor_reduce(dr[:], pages(drr[:]), AXIS_X, ALU.add)
        q0_s = small("q0_s")
        nc.vector.tensor_tensor(q0_s[:], q0[:], inv_s[:], ALU.mult)
        sig_sq_s = small("sig_sq_s")
        nc.vector.tensor_tensor(sig_sq_s[:], sig_sq[:], inv_s[:], ALU.mult)
        neg_p = small("neg_p", 1)
        nc.scalar.activation(neg_p[:], sig_sq_sum[:], ACT.Copy, scale=neg_inv_z[:])
        gain = small("gain", 1)
        nc.scalar.activation(gain[:], neg_inv_z[:], ACT.Square, scale=math.sqrt(GAIN))

        terms = small("terms")
        neg_mu = small("neg_mu", 1)
        nc.vector.scalar_tensor_tensor(terms[:], dr[:], neg_inv_z[:], q0_s[:], ALU.mult, ALU.mult, accum_out=neg_mu[:])
        u = small("u")
        nc.vector.tensor_tensor(u[:], dr[:], inv_s[:], ALU.mult)
        terms2 = small("terms2")
        neg_b = small("neg_b", 1)
        nc.vector.scalar_tensor_tensor(terms2[:], dr[:], neg_inv_z[:], sig_sq_s[:], ALU.mult, ALU.mult, accum_out=neg_b[:])
        v = small("v")
        nc.vector.scalar_tensor_tensor(v[:], u[:], neg_mu[:], sig[:], ALU.add, ALU.mult)
        vo = small("vo")
        nc.vector.scalar_tensor_tensor(vo[:], u[:], neg_mu[:], slope[:], ALU.add, ALU.mult)
        neg_s1 = small("neg_s1", 1)
        nc.vector.tensor_scalar(neg_s1[:], neg_p[:], neg_mu[:], neg_b[:], ALU.mult, ALU.add)
        terms3 = small("terms3")
        neg_s2 = small("neg_s2", 1)
        nc.vector.scalar_tensor_tensor(terms3[:], v[:], neg_inv_z[:], v[:], ALU.mult, ALU.mult, accum_out=neg_s2[:])
        own = small("own")
        nc.vector.scalar_tensor_tensor(own[:], vo[:], neg_s1[:], v[:], ALU.add, ALU.mult)
        e = small("e")
        nc.vector.scalar_tensor_tensor(e[:], sig[:], neg_s2[:], own[:], ALU.mult, ALU.add)

        for h, queue in enumerate((nc.sync, nc.scalar)):
            result = sb.tile([P, I // 2], F32, name="result%d" % h)
            nc.vector.scalar_tensor_tensor(
                pages(result[:]), spread(e[:, PAGE_HALVES[h]]), gain[:],
                pages(base_sb[:, SLOT_HALVES[h]]), ALU.mult, ALU.add,
            )
            queue.dma_start(out[:, SLOT_HALVES[h]], result[:])
